import numpy as np
import ml_dtypes


def mxq(x, axis, fmt="e4m3"):
    dtype, down = {"e4m3": (ml_dtypes.float8_e4m3fn, 7), "e5m2": (ml_dtypes.float8_e5m2, 14)}[fmt]
    v = np.moveaxis(np.asarray(x, np.float32).astype(ml_dtypes.bfloat16).astype(np.float64), axis, -1)
    blocks = v.reshape(v.shape[:-1] + (-1, 32))
    amax = np.abs(blocks).max(-1, keepdims=True)
    byte = np.maximum(np.where(amax > 0, np.frexp(amax)[1] - 1 + 127, 0) - down, 1)
    scale = np.exp2(byte - 127.0)
    codes = (blocks / scale).astype(np.float32).astype(dtype).astype(np.float64)
    return np.moveaxis((codes * scale).reshape(v.shape), -1, axis)


WIDE = False


def mx_kscale(k):
    if not WIDE:
        return np.ones(k)
    levels = np.array([10, -10, 5, -5, 0])
    if k % 512:
        return np.exp2(np.random.permutation(np.resize(levels, k // 32))).repeat(32)
    a = np.empty((k // 512, 16))
    for p in range(k // 512):
        a[p, :8] = np.random.permutation(np.resize(levels, 8))
        for g in range(8):
            far = levels[np.abs(levels - a[p, g]) >= 10]
            a[p, g + 8] = far[np.random.randint(len(far))]
    return np.exp2(a.ravel()).repeat(32)


def f64(x):
    return np.asarray(x).astype(np.float64)


def striped(idx):
    return np.tile(idx.reshape(-1, 16).T, (8, 1)).astype(np.uint16)


def unstriped(offs):
    return offs[:16].T.reshape(-1).astype(np.int64)


def pack_weight(w):
    k, n = w.shape
    w = f64(np.asarray(w, np.float32).astype(ml_dtypes.bfloat16)).reshape(k // 32, 32, n)
    amax = np.abs(w).max(1)
    byte = np.clip(np.where(amax > 0, np.frexp(amax)[1] - 1 + 127 - 7, 1), 1, 254)
    scaled = (w * np.exp2(127.0 - byte)[:, None, :]).reshape(k, n).astype(np.float32)
    words = np.ascontiguousarray(scaled.reshape(k // 512, 128, 4, n).transpose(0, 1, 3, 2)).astype(ml_dtypes.float8_e4m3fn).view(np.uint8)
    return words, np.ascontiguousarray(byte.astype(np.uint8).reshape(k // 512, 16, n))


def unpack_weight(words, scales):
    g, p, n, _ = words.shape
    vals = np.ascontiguousarray(words).view(ml_dtypes.float8_e4m3fn).astype(np.float64) * np.repeat(np.exp2(scales.astype(np.float64) - 127.0), 8, axis=1)[..., None]
    return vals.transpose(0, 1, 3, 2).reshape(g * 512, n)


def planes(y):
    n, m = y.shape
    v = y.astype(np.float32).astype(ml_dtypes.bfloat16).astype(np.float64).reshape(n // 32, 32, m)
    top = np.abs(v).max(1)
    byte = np.clip(np.where(top > 0, np.frexp(top)[1] - 1 + 127 - 7, 1), 1, 254)
    codes = (v * np.exp2(127.0 - byte)[:, None, :]).reshape(n, m).astype(np.float32).astype(ml_dtypes.float8_e4m3fn).view(np.uint8)
    words = codes.reshape(n // 512, 128, 4, m).transpose(0, 1, 3, 2)
    return np.ascontiguousarray(words), np.ascontiguousarray(byte.astype(np.uint8).reshape(n // 512, 16, m))


K, T, S, N, H, W, U = 512, 2048, 512, 512, 512, 2048, 1024


def setup_inputs():
    n = np.random.standard_normal
    s = mx_kscale(K)[:, None]
    u = mx_kscale(H)
    packed_xT = pack_weight(n((K, T)) * s)
    packed_eT = pack_weight(n((K, W)) * s)
    return {
        "x_words": packed_xT[0],
        "x_scales": packed_xT[1],
        "w1": (n((K, N)) / np.sqrt(K) / s).astype(np.float32),
        "e_words": packed_eT[0],
        "e_scales": packed_eT[1],
        "w2": (n((K, N)) / np.sqrt(K) / s).astype(np.float32),
        "unit": (np.random.uniform(0.6, 1.4, (H, 1)) * u[:, None]).astype(np.float32),
        "w3": (n((H, N)) / np.sqrt(H) / u[:, None]).astype(np.float32),
        "offs": striped(np.random.permutation(T)[:S]),
        "doc": striped(np.random.permutation(W)[:S]),
        "qa": striped(np.random.permutation(np.concatenate([np.arange(S), np.random.randint(0, S, U - S)]))),
        "qb": striped(np.random.permutation(np.concatenate([np.arange(S), np.random.randint(0, S, U - S)]))),
        "da": striped(np.random.permutation(np.concatenate([np.arange(S), np.random.randint(0, S, U - S)]))),
        "db": striped(np.random.permutation(np.concatenate([np.arange(S), np.random.randint(0, S, U - S)]))),
    }


def reference(x_words, x_scales, w1, e_words, e_scales, w2, unit, w3, offs, doc, qa, qb, da, db):
    xq = unpack_weight(x_words, x_scales)[:, unstriped(offs)]
    y = mxq(f64(w1), 0, "e4m3").T @ xq
    y_1 = y[:, unstriped(qa)]
    e_doc = unpack_weight(e_words, e_scales)[:, unstriped(doc)]
    ye = mxq(f64(w2), 0, "e4m3").T @ e_doc
    e_1 = ye[:, unstriped(da)]
    y_2 = y[:, unstriped(qb)]
    e_2 = ye[:, unstriped(db)]
    hid = f64(unit) * np.maximum(y_1 * e_1, y_2 * e_2)
    out_0 = mxq(f64(w3), 0, "e4m3").T @ mxq(hid, 0, "e4m3")
    return (out_0,) + planes(out_0)

@@ -1,0 +1,228 @@
+from contextlib import ExitStack
+
+import concourse.mybir as mybir
+
+K, T, S, U = 512, 2048, 512, 1024
+FLOPS = 2 * K * 512 * S * 2 + 2 * 512 * 512 * U
+
+F32 = mybir.dt.float32
+BF16 = mybir.dt.bfloat16
+I32 = mybir.dt.int32
+U32 = mybir.dt.uint32
+U16 = mybir.dt.uint16
+U8 = mybir.dt.uint8
+FP8X4 = mybir.dt.float8_e4m3fn_x4
+ALU = mybir.AluOpType
+COPY = mybir.ActivationFunctionType.Copy
+
+P = 128
+PACK = 4
+HALF = 256
+GROUP = 128
+CHUNKS = (384, 256, 256, 128)
+EARLY = 4
+
+
+def tile_picked_ydocqa_max_po_kernel(
+    tc, x_words, x_scales, w1, e_words, e_scales, w2, unit, w3, offs, doc, qa, qb, da, db, out_0, out_1, out_2
+):
+    nc = tc.nc
+    with ExitStack() as ctx:
+        keep = ctx.enter_context(tc.tile_pool(name="keep", bufs=1))
+        psum = ctx.enter_context(tc.psum_pool(name="psum", bufs=1))
+
+        def load_list(name, src):
+            tile = keep.tile([P, src.shape[1]], U16, name=name)
+            nc.sync.dma_start(tile[:], src)
+            return tile
+
+        def load_words(name, src):
+            tile = keep.tile([P, T], U32, name=name)
+            nc.sync.dma_start(tile[:].bitcast(I32), src[0].rearrange("p n t -> p (n t)").bitcast(I32))
+            return tile
+
+        def cleared(name):
+            tile = keep.tile([P, T], U8, name=name)
+            nc.vector.memset(tile[:].bitcast(I32), 0)
+            return tile
+
+        def load_scales(tile, src):
+            for q in range(4):
+                nc.sync.dma_start(tile[32 * q : 32 * q + 4, :].bitcast(I32), src[0, 4 * q : 4 * q + 4, :].bitcast(I32))
+
+        def load_weight_half(name, src, h):
+            tile = keep.tile([P, PACK, HALF], F32, name=name)
+            nc.sync.dma_start(tile[:], src.rearrange("(p j) c -> p j c", j=PACK)[:, :, h * HALF : (h + 1) * HALF])
+            return tile
+
+        x_sc = cleared("x_sc")
+        e_sc = cleared("e_sc")
+        offs_t = load_list("offs_t", offs)
+        doc_t = load_list("doc_t", doc)
+        qa_t = load_list("qa_t", qa)
+        u_t = keep.tile([P, PACK], F32, name="u_t")
+        nc.sync.dma_start(u_t[:], unit.rearrange("(p t) o -> p (t o)", t=PACK))
+        x_wd = load_words("x_wd", x_words)
+        load_scales(x_sc, x_scales)
+        w1_raw = [load_weight_half("w1a", w1, 0), load_weight_half("w1b", w1, 1)]
+        load_scales(e_sc, e_scales)
+        e_wd = load_words("e_wd", e_words)
+        qb_t = load_list("qb_t", qb)
+        w2_raw = [load_weight_half("w2a", w2, 0), load_weight_half("w2b", w2, 1)]
+        da_t = load_list("da_t", da)
+        db_t = load_list("db_t", db)
+        w3_raw = keep.tile([P, PACK, 512], F32, name="w3_raw")
+        nc.sync.dma_start(w3_raw[:], w3.rearrange("(p j) c -> p j c", j=PACK))
+
+        banks = [psum.tile([P, 512], F32, name="bank%d" % b) for b in range(8)]
+
+        def dealt_out(grouped, m0, m1):
+            return grouped[:].rearrange("p (t m j) -> p m j t", t=PACK, j=PACK)[:, m0:m1]
+
+        def dealt_in(raw):
+            return raw[:].rearrange("p j (m t) -> p m j t", t=PACK)
+
+        def quantize(name, grouped, width):
+            codes = keep.tile([P, width], U32, name=name + "_codes", align_bytes=64)
+            scales = keep.tile([P, width], U8, name=name + "_scales", align_bytes=64)
+            nc.vector.quantize_mx(out=codes[:].bitcast(FP8X4), scales=scales[:], in_=grouped)
+            return codes, scales
+
+        def quantize_weight(name, grouped):
+            codes = keep.tile([P, 512], U32, name=name + "_codes", align_bytes=64)
+            scales = keep.tile([P, 512], U8, name=name + "_scales", align_bytes=64)
+            for t in range(PACK):
+                cols = slice(t * P, (t + 1) * P)
+                nc.vector.quantize_mx(out=codes[:, cols].bitcast(FP8X4), scales=scales[:, cols], in_=grouped[:, t * 512 : (t + 1) * 512])
+            return codes, scales
+
+        def pick(name, table, lst, dtype):
+            tile = keep.tile([P, S], dtype, name=name, align_bytes=64)
+            nc.vector.tensor_copy(tile[:], table[:].indirect(lst[:]))
+            return tile
+
+        def product(dst, w, t, codes, scales):
+            nc.tensor.matmul_mx(
+                out=dst,
+                lhsT=w[0][:, t * P : (t + 1) * P].bitcast(FP8X4),
+                lhsT_scale=w[1][:, t * P : (t + 1) * P],
+                rhs=codes.bitcast(FP8X4),
+                rhs_scale=scales,
+                start=True,
+                stop=True,
+            )
+
+        w1_g = keep.tile([P, PACK * 512], BF16, name="w1_g", align_bytes=64)
+        for h in range(2):
+            nc.scalar.copy(dealt_out(w1_g, 64 * h, 64 * h + 64), dealt_in(w1_raw[h]))
+        xw_pick = pick("xw_pick", x_wd, offs_t, U32)
+        xs_pick = pick("xs_pick", x_sc, offs_t, U8)
+        w1_q = quantize_weight("w1", w1_g)
+        y = []
+        for t in range(PACK):
+            product(banks[t][:], w1_q, t, xw_pick[:], xs_pick[:])
+            yt = keep.tile([P, S], F32, name="y%d" % t)
+            if t < 2:
+                nc.scalar.copy(yt[:], banks[t][:])
+            y.append(yt)
+
+        es_pick = pick("es_pick", e_sc, doc_t, U8)
+        ew_pick = pick("ew_pick", e_wd, doc_t, U32)
+        sign = keep.tile([P, PACK], F32, name="sign")
+        half = keep.tile([P, PACK], F32, name="half")
+        size = keep.tile([P, PACK], F32, name="size", tag="late")
+        nc.vector.tensor_scalar(half[:], u_t[:], 0.0, 0.5, ALU.is_ge, ALU.subtract)
+        w2_g = keep.tile([P, PACK * 512], BF16, name="w2_g", align_bytes=64)
+        nc.vector.tensor_copy(dealt_out(w2_g, 0, 64), dealt_in(w2_raw[0]))
+        nc.vector.tensor_scalar(sign[:], half[:], 2.0, None, ALU.mult)
+        nc.vector.tensor_copy(dealt_out(w2_g, 64, 128), dealt_in(w2_raw[1]))
+        nc.vector.tensor_tensor(size[:], u_t[:], sign[:], ALU.mult)
+        w2_q = quantize_weight("w2", w2_g)
+        ye = []
+        for t in range(PACK):
+            product(banks[PACK + t][:], w2_q, t, ew_pick[:], es_pick[:])
+            yt = keep.tile([P, S], F32, name="ye%d" % t)
+            if t == 0:
+                nc.vector.tensor_scalar(yt[:], banks[PACK + t][:], size[:, t : t + 1], None, ALU.mult)
+            else:
+                nc.scalar.activation(yt[:], banks[PACK + t][:], COPY, scale=size[:, t : t + 1])
+            ye.append(yt)
+        for t in range(2, PACK):
+            nc.vector.tensor_copy(y[t][:], banks[t][:])
+        early = EARLY * CHUNKS[0]
+        g_early = keep.tile([P, early], F32, name="g_early")
+        g_late = keep.tile([P, 2 * PACK * U - early], F32, name="g_late", tag="late")
+        w3_g = keep.tile([P, PACK * 512], BF16, name="w3_g", align_bytes=64)
+
+        def round_w3():
+            for h in range(2):
+                nc.vector.tensor_tensor(
+                    dealt_out(w3_g, 64 * h, 64 * h + 64),
+                    dealt_in(w3_raw)[:, 64 * h : 64 * h + 64],
+                    sign[:].unsqueeze(1).unsqueeze(3).to_broadcast([P, 64, PACK, PACK]),
+                    ALU.mult,
+                )
+
+        out_scales = keep.tile([P, U], U8, name="out_scales", align_bytes=64)
+        out_rows = out_0.rearrange("(p t) r -> p t r", t=PACK)
+        out_words = out_1[0].rearrange("p n t -> p (n t)").bitcast(I32)
+        starts = [sum(CHUNKS[:c]) for c in range(len(CHUNKS))]
+
+        def woven(tile):
+            return tile[:].rearrange("p (c i t) -> p c t i", i=4, t=PACK)
+
+        def planes(tile):
+            return tile[:].rearrange("p t (c i) -> p c t i", i=4)
+
+        def front(c):
+            r0, n = starts[c], CHUNKS[c]
+            cols = slice(r0 // 16, (r0 + n) // 16)
+            prods = [keep.tile([P, PACK, n], F32, name="p%s%d" % (name, c)) for name in ("a", "b")]
+            for t in range(PACK):
+                for s, (ql, dl) in enumerate(((qa_t, da_t), (qb_t, db_t))):
+                    at = 2 * PACK * r0 + (2 * t + s) * n
+                    g = g_early[:, at : at + n] if at < early else g_late[:, at - early : at - early + n]
+                    nc.scalar.activation(g, y[t][:].indirect(ql[:, cols]), COPY)
+                    nc.vector.tensor_tensor(prods[s][:, t, :], ye[t][:].indirect(dl[:, cols]), g, ALU.mult)
+                if c == 0 and t == 1:
+                    round_w3()
+            hid = keep.tile([P, PACK * n], BF16, name="hid%d" % c, align_bytes=64)
+            nc.vector.tensor_tensor(woven(hid), planes(prods[0]), planes(prods[1]), ALU.max)
+            return hid
+
+        def middle(c, hid, w3_q):
+            r0, n = starts[c], CHUNKS[c]
+            codes, scales = quantize("hid%d" % c, hid[:], n)
+            res = keep.tile([P, PACK, n], F32, name="res%d" % c)
+            for g0 in range(0, n, GROUP):
+                bank = banks[(r0 + g0) // GROUP]
+                for t in range(PACK):
+                    product(bank[:, t * GROUP : (t + 1) * GROUP], w3_q, t, codes[:, g0 : g0 + GROUP], scales[:, g0 : g0 + GROUP])
+                nc.scalar.copy(res[:, :, g0 : g0 + GROUP], bank[:].rearrange("p (t r) -> p t r", t=PACK))
+            nc.sync.dma_start(out_rows[:, :, r0 : r0 + n], res[:])
+            rounded = keep.tile([P, PACK * n], BF16, name="rounded%d" % c, align_bytes=64)
+            if c == len(CHUNKS) - 1:
+                nc.vector.tensor_copy(woven(rounded), planes(res))
+            else:
+                nc.scalar.copy(woven(rounded), planes(res))
+            return rounded
+
+        def back(c, rounded):
+            r0, n = starts[c], CHUNKS[c]
+            codes = keep.tile([P, n], U32, name="out_codes%d" % c, align_bytes=64)
+            nc.vector.quantize_mx(out=codes[:].bitcast(FP8X4), scales=out_scales[:, r0 : r0 + n], in_=rounded[:])
+            nc.sync.dma_start(out_words[:, r0 : r0 + n], codes[:].bitcast(I32))
+
+        hid = front(0)
+        w3_q = quantize("w3", w3_g[:], 512)
+        rounded = []
+        for c in range(len(CHUNKS)):
+            rounded.append(middle(c, hid, w3_q))
+            if c + 1 < len(CHUNKS):
+                hid = front(c + 1)
+            if c > 0:
+                back(c - 1, rounded[c - 1])
+        back(len(CHUNKS) - 1, rounded[-1])
+        for q in range(4):
+            eng = nc.sync if q % 2 == 0 else nc.scalar
+            eng.dma_start(out_2[0, 4 * q : 4 * q + 4, :].bitcast(I32), out_scales[32 * q : 32 * q + 4, :].bitcast(I32))

@@ -19,8 +19,10 @@ P = 128
 PACK = 4
 HALF = 256
 GROUP = 128
-CHUNKS = (384, 256, 256, 128)
-EARLY = 4
+CHUNKS = (512, 384, 128)
+EARLY = 3
+SPARE = 16
+E_ROW = 8
 
 
 def tile_picked_ydocqa_max_po_kernel(
@@ -46,9 +48,9 @@ def tile_picked_ydocqa_max_po_kernel(
             nc.vector.memset(tile[:].bitcast(I32), 0)
             return tile
 
-        def load_scales(tile, src):
+        def load_scales(tile, src, row):
             for q in range(4):
-                nc.sync.dma_start(tile[32 * q : 32 * q + 4, :].bitcast(I32), src[0, 4 * q : 4 * q + 4, :].bitcast(I32))
+                nc.sync.dma_start(tile[32 * q + row : 32 * q + row + 4, :].bitcast(I32), src[0, 4 * q : 4 * q + 4, :].bitcast(I32))
 
         def load_weight_half(name, src, h):
             tile = keep.tile([P, PACK, HALF], F32, name=name)
@@ -63,9 +65,9 @@ def tile_picked_ydocqa_max_po_kernel(
         u_t = keep.tile([P, PACK], F32, name="u_t")
         nc.sync.dma_start(u_t[:], unit.rearrange("(p t) o -> p (t o)", t=PACK))
         x_wd = load_words("x_wd", x_words)
-        load_scales(x_sc, x_scales)
+        load_scales(x_sc, x_scales, 0)
         w1_raw = [load_weight_half("w1a", w1, 0), load_weight_half("w1b", w1, 1)]
-        load_scales(e_sc, e_scales)
+        load_scales(e_sc, e_scales, E_ROW)
         e_wd = load_words("e_wd", e_words)
         qb_t = load_list("qb_t", qb)
         w2_raw = [load_weight_half("w2a", w2, 0), load_weight_half("w2b", w2, 1)]
@@ -96,6 +98,11 @@ def tile_picked_ydocqa_max_po_kernel(
                 nc.vector.quantize_mx(out=codes[:, cols].bitcast(FP8X4), scales=scales[:, cols], in_=grouped[:, t * 512 : (t + 1) * 512])
             return codes, scales
 
+        def window(name):
+            tile = keep.tile([P, S + SPARE], F32, name=name)
+            nc.gpsimd.memset(tile[:, S:], 0.0)
+            return tile
+
         def pick(name, table, lst, dtype):
             tile = keep.tile([P, S], dtype, name=name, align_bytes=64)
             nc.vector.tensor_copy(tile[:], table[:].indirect(lst[:]))
@@ -113,17 +120,16 @@ def tile_picked_ydocqa_max_po_kernel(
             )
 
         w1_g = keep.tile([P, PACK * 512], BF16, name="w1_g", align_bytes=64)
-        for h in range(2):
-            nc.scalar.copy(dealt_out(w1_g, 64 * h, 64 * h + 64), dealt_in(w1_raw[h]))
+        nc.scalar.copy(dealt_out(w1_g, 0, 64), dealt_in(w1_raw[0]))
         xw_pick = pick("xw_pick", x_wd, offs_t, U32)
         xs_pick = pick("xs_pick", x_sc, offs_t, U8)
+        nc.vector.tensor_copy(dealt_out(w1_g, 64, 128), dealt_in(w1_raw[1]))
         w1_q = quantize_weight("w1", w1_g)
         y = []
         for t in range(PACK):
             product(banks[t][:], w1_q, t, xw_pick[:], xs_pick[:])
-            yt = keep.tile([P, S], F32, name="y%d" % t)
-            if t < 2:
-                nc.scalar.copy(yt[:], banks[t][:])
+            yt = window("y%d" % t)
+            nc.scalar.copy(yt[:, :S], banks[t][:])
             y.append(yt)
 
         es_pick = pick("es_pick", e_sc, doc_t, U8)
@@ -131,24 +137,22 @@ def tile_picked_ydocqa_max_po_kernel(
         sign = keep.tile([P, PACK], F32, name="sign")
         half = keep.tile([P, PACK], F32, name="half")
         size = keep.tile([P, PACK], F32, name="size", tag="late")
-        nc.vector.tensor_scalar(half[:], u_t[:], 0.0, 0.5, ALU.is_ge, ALU.subtract)
+        nc.gpsimd.tensor_scalar(half[:], u_t[:], 0.0, 0.5, ALU.is_ge, ALU.subtract)
         w2_g = keep.tile([P, PACK * 512], BF16, name="w2_g", align_bytes=64)
         nc.vector.tensor_copy(dealt_out(w2_g, 0, 64), dealt_in(w2_raw[0]))
-        nc.vector.tensor_scalar(sign[:], half[:], 2.0, None, ALU.mult)
+        nc.gpsimd.tensor_scalar(sign[:], half[:], 2.0, 0.0, ALU.mult, ALU.add)
         nc.vector.tensor_copy(dealt_out(w2_g, 64, 128), dealt_in(w2_raw[1]))
-        nc.vector.tensor_tensor(size[:], u_t[:], sign[:], ALU.mult)
+        nc.gpsimd.tensor_tensor(size[:], u_t[:], sign[:], ALU.mult)
         w2_q = quantize_weight("w2", w2_g)
         ye = []
         for t in range(PACK):
-            product(banks[PACK + t][:], w2_q, t, ew_pick[:], es_pick[:])
-            yt = keep.tile([P, S], F32, name="ye%d" % t)
+            product(banks[PACK + t][:], w2_q, t, ew_pick[:], es_pick[E_ROW:P, :])
+            yt = window("ye%d" % t)
             if t == 0:
-                nc.vector.tensor_scalar(yt[:], banks[PACK + t][:], size[:, t : t + 1], None, ALU.mult)
+                nc.vector.tensor_scalar(yt[:, :S], banks[PACK + t][:], size[:, t : t + 1], None, ALU.mult)
             else:
-                nc.scalar.activation(yt[:], banks[PACK + t][:], COPY, scale=size[:, t : t + 1])
+                nc.scalar.activation(yt[:, :S], banks[PACK + t][:], COPY, scale=size[:, t : t + 1])
             ye.append(yt)
-        for t in range(2, PACK):
-            nc.vector.tensor_copy(y[t][:], banks[t][:])
         early = EARLY * CHUNKS[0]
         g_early = keep.tile([P, early], F32, name="g_early")
         g_late = keep.tile([P, 2 * PACK * U - early], F32, name="g_late", tag="late")
@@ -169,42 +173,69 @@ def tile_picked_ydocqa_max_po_kernel(
         starts = [sum(CHUNKS[:c]) for c in range(len(CHUNKS))]
 
         def woven(tile):
-            return tile[:].rearrange("p (c i t) -> p c t i", i=4, t=PACK)
+            return tile[:].rearrange("p (c i t) -> p c t i", i=2, t=PACK)
 
         def planes(tile):
-            return tile[:].rearrange("p t (c i) -> p c t i", i=4)
+            return tile.rearrange("p t (c i) -> p c t i", i=2)
+
+        def gathered(t, s, r0, n):
+            at = (r0 // S) * 2 * PACK * S + (2 * t + s) * S + r0 % S
+            return g_early[:, at : at + n] if at < early else g_late[:, at - early : at - early + n]
+
+        def fetch_questions(r0):
+            cols = slice(r0 // 16, (r0 + S) // 16)
+            for t in range(PACK):
+                for s, ql in enumerate((qa_t, qb_t)):
+                    nc.scalar.activation(gathered(t, s, r0, S), y[t][:].indirect(ql[:, cols]), COPY)
 
         def front(c):
             r0, n = starts[c], CHUNKS[c]
             cols = slice(r0 // 16, (r0 + n) // 16)
-            prods = [keep.tile([P, PACK, n], F32, name="p%s%d" % (name, c)) for name in ("a", "b")]
-            for t in range(PACK):
-                for s, (ql, dl) in enumerate(((qa_t, da_t), (qb_t, db_t))):
-                    at = 2 * PACK * r0 + (2 * t + s) * n
-                    g = g_early[:, at : at + n] if at < early else g_late[:, at - early : at - early + n]
-                    nc.scalar.activation(g, y[t][:].indirect(ql[:, cols]), COPY)
-                    nc.vector.tensor_tensor(prods[s][:, t, :], ye[t][:].indirect(dl[:, cols]), g, ALU.mult)
-                if c == 0 and t == 1:
-                    round_w3()
+            prods = keep.tile([P, 2, PACK, n], F32, name="prods%d" % c, tag="hid1" if c == 2 else "prods%d" % c, align_bytes=64)
+            if r0 % S == 0:
+                fetch_questions(r0)
+            if c < len(CHUNKS) - 1:
+                for t in range(PACK):
+                    for s, dl in enumerate((da_t, db_t)):
+                        nc.vector.tensor_tensor(prods[:, s, t, :], ye[t][:].indirect(dl[:, cols]), gathered(t, s, r0, n), ALU.mult)
+                    if c == 0 and t == 1:
+                        round_w3()
+            else:
+                docs = keep.tile([P, PACK, 2, n], F32, name="docs")
+                for t in range(PACK):
+                    for s, dl in enumerate((da_t, db_t)):
+                        nc.scalar.activation(docs[:, t, s, :], ye[t][:].indirect(dl[:, cols]), COPY)
+                base = (r0 // S) * 2 * PACK * S - early
+                qs = g_late[:, base : base + 2 * PACK * S].rearrange("p (t s r) -> p t s r", t=PACK, s=2)[:, :, :, r0 % S : r0 % S + n]
+                nc.vector.tensor_tensor(prods[:].rearrange("p s t r -> p t s r"), docs[:], qs, ALU.mult)
             hid = keep.tile([P, PACK * n], BF16, name="hid%d" % c, align_bytes=64)
-            nc.vector.tensor_tensor(woven(hid), planes(prods[0]), planes(prods[1]), ALU.max)
+            nc.vector.tensor_tensor(woven(hid), planes(prods[:, 0]), planes(prods[:, 1]), ALU.max)
             return hid
 
         def middle(c, hid, w3_q):
             r0, n = starts[c], CHUNKS[c]
             codes, scales = quantize("hid%d" % c, hid[:], n)
             res = keep.tile([P, PACK, n], F32, name="res%d" % c)
-            for g0 in range(0, n, GROUP):
-                bank = banks[(r0 + g0) // GROUP]
+            if n == GROUP:
                 for t in range(PACK):
-                    product(bank[:, t * GROUP : (t + 1) * GROUP], w3_q, t, codes[:, g0 : g0 + GROUP], scales[:, g0 : g0 + GROUP])
-                nc.scalar.copy(res[:, :, g0 : g0 + GROUP], bank[:].rearrange("p (t r) -> p t r", t=PACK))
-            nc.sync.dma_start(out_rows[:, :, r0 : r0 + n], res[:])
-            rounded = keep.tile([P, PACK * n], BF16, name="rounded%d" % c, align_bytes=64)
-            if c == len(CHUNKS) - 1:
-                nc.vector.tensor_copy(woven(rounded), planes(res))
+                    product(banks[0][:, t * n : (t + 1) * n], w3_q, t, codes[:], scales[:])
+                nc.scalar.copy(res[:], banks[0][:].rearrange("p (t r) -> p t r", t=PACK))
             else:
-                nc.scalar.copy(woven(rounded), planes(res))
+                for t in range(PACK):
+                    bank = banks[PACK * c + t]
+                    for g0, g1 in ((0, n),) if n == 512 else ((0, 256), (256, n)):
+                        product(bank[:, g0:g1], w3_q, t, codes[:, g0:g1], scales[:, g0:g1])
+                    nc.scalar.copy(res[:, t, :], bank[:, :n])
+            nc.sync.dma_start(out_rows[:, :, r0 : r0 + n], res[:])
+            return res
+
+        def round_result(c, res):
+            n = CHUNKS[c]
+            rounded = keep.tile([P, PACK * n], BF16, name="rounded%d" % c, align_bytes=64)
+            if c == 0:
+                nc.scalar.copy(woven(rounded), planes(res[:]))
+            else:
+                nc.vector.tensor_copy(woven(rounded), planes(res[:]))
             return rounded
 
         def back(c, rounded):
@@ -215,14 +246,13 @@ def tile_picked_ydocqa_max_po_kernel(
 
         hid = front(0)
         w3_q = quantize("w3", w3_g[:], 512)
-        rounded = []
-        for c in range(len(CHUNKS)):
-            rounded.append(middle(c, hid, w3_q))
-            if c + 1 < len(CHUNKS):
-                hid = front(c + 1)
-            if c > 0:
-                back(c - 1, rounded[c - 1])
-        back(len(CHUNKS) - 1, rounded[-1])
+        res0 = middle(0, hid, w3_q)
+        rounded0 = round_result(0, res0)
+        res1 = middle(1, front(1), w3_q)
+        res2 = middle(2, front(2), w3_q)
+        back(0, rounded0)
+        back(1, round_result(1, res1))
+        back(2, round_result(2, res2))
         for q in range(4):
             eng = nc.sync if q % 2 == 0 else nc.scalar
             eng.dma_start(out_2[0, 4 * q : 4 * q + 4, :].bitcast(I32), out_scales[32 * q : 32 * q + 4, :].bitcast(I32))

@@ -226,21 +226,25 @@ def tile_picked_ydocqa_max_po_kernel(
                     for g0, g1 in ((0, n),) if n == 512 else ((0, 256), (256, n)):
                         product(bank[:, g0:g1], w3_q, t, codes[:, g0:g1], scales[:, g0:g1])
                     nc.scalar.copy(res[:, t, :], bank[:, :n])
-            nc.sync.dma_start(out_rows[:, :, r0 : r0 + n], res[:])
+                    if c == 1 and t % 2 == 1:
+                        nc.sync.dma_start(out_rows[:, t - 1 : t + 1, r0 : r0 + n], res[:, t - 1 : t + 1, :])
+            if c != 1:
+                nc.sync.dma_start(out_rows[:, :, r0 : r0 + n], res[:])
             return res
 
         def round_result(c, res):
             n = CHUNKS[c]
             rounded = keep.tile([P, PACK * n], BF16, name="rounded%d" % c, align_bytes=64)
-            if c == 0:
-                nc.scalar.copy(woven(rounded), planes(res[:]))
-            else:
-                nc.vector.tensor_copy(woven(rounded), planes(res[:]))
+            cut = (n, 256, 0)[c] // 2
+            if cut > 0:
+                nc.scalar.copy(woven(rounded)[:, :cut], planes(res[:])[:, :cut])
+            if cut < n // 2:
+                nc.vector.tensor_copy(woven(rounded)[:, cut:], planes(res[:])[:, cut:])
             return rounded
 
         def back(c, rounded):
             r0, n = starts[c], CHUNKS[c]
-            codes = keep.tile([P, n], U32, name="out_codes%d" % c, align_bytes=64)
+            codes = keep.tile([P, n], U32, name="out_codes%d" % c, tag="hid2" if c == 0 else "out_codes%d" % c, align_bytes=64)
             nc.vector.quantize_mx(out=codes[:].bitcast(FP8X4), scales=out_scales[:, r0 : r0 + n], in_=rounded[:])
             nc.sync.dma_start(out_words[:, r0 : r0 + n], codes[:].bitcast(I32))
 

@@ -59,14 +59,15 @@ def tile_picked_ydocqa_max_po_kernel(
 
         x_sc = cleared("x_sc")
         e_sc = cleared("e_sc")
+        x_wd = load_words("x_wd", x_words)
         offs_t = load_list("offs_t", offs)
-        doc_t = load_list("doc_t", doc)
-        qa_t = load_list("qa_t", qa)
         u_t = keep.tile([P, PACK], F32, name="u_t")
         nc.sync.dma_start(u_t[:], unit.rearrange("(p t) o -> p (t o)", t=PACK))
-        x_wd = load_words("x_wd", x_words)
+        w1_raw = [load_weight_half("w1a", w1, 0)]
         load_scales(x_sc, x_scales, 0)
-        w1_raw = [load_weight_half("w1a", w1, 0), load_weight_half("w1b", w1, 1)]
+        w1_raw.append(load_weight_half("w1b", w1, 1))
+        doc_t = load_list("doc_t", doc)
+        qa_t = load_list("qa_t", qa)
         load_scales(e_sc, e_scales, E_ROW)
         e_wd = load_words("e_wd", e_words)
         qb_t = load_list("qb_t", qb)

from contextlib import ExitStack

import concourse.mybir as mybir

K, T, S, U = 512, 2048, 512, 1024
FLOPS = 2 * K * 512 * S * 2 + 2 * 512 * 512 * U

F32 = mybir.dt.float32
BF16 = mybir.dt.bfloat16
I32 = mybir.dt.int32
U32 = mybir.dt.uint32
U16 = mybir.dt.uint16
U8 = mybir.dt.uint8
FP8X4 = mybir.dt.float8_e4m3fn_x4
ALU = mybir.AluOpType
COPY = mybir.ActivationFunctionType.Copy

P = 128
PACK = 4
HALF = 256
GROUP = 128
CHUNKS = (512, 384, 128)
EARLY = 3
SPARE = 16
E_ROW = 8


def tile_picked_ydocqa_max_po_kernel(
    tc, x_words, x_scales, w1, e_words, e_scales, w2, unit, w3, offs, doc, qa, qb, da, db, out_0, out_1, out_2
):
    nc = tc.nc
    with ExitStack() as ctx:
        keep = ctx.enter_context(tc.tile_pool(name="keep", bufs=1))
        psum = ctx.enter_context(tc.psum_pool(name="psum", bufs=1))

        def load_list(name, src):
            tile = keep.tile([P, src.shape[1]], U16, name=name)
            nc.sync.dma_start(tile[:], src)
            return tile

        def load_words(name, src):
            tile = keep.tile([P, T], U32, name=name)
            nc.sync.dma_start(tile[:].bitcast(I32), src[0].rearrange("p n t -> p (n t)").bitcast(I32))
            return tile

        def cleared(name):
            tile = keep.tile([P, T], U8, name=name)
            nc.vector.memset(tile[:].bitcast(I32), 0)
            return tile

        def load_scales(tile, src, row):
            for q in range(4):
                nc.sync.dma_start(tile[32 * q + row : 32 * q + row + 4, :].bitcast(I32), src[0, 4 * q : 4 * q + 4, :].bitcast(I32))

        def load_weight_half(name, src, h):
            tile = keep.tile([P, PACK, HALF], F32, name=name)
            nc.sync.dma_start(tile[:], src.rearrange("(p j) c -> p j c", j=PACK)[:, :, h * HALF : (h + 1) * HALF])
            return tile

        x_sc = cleared("x_sc")
        e_sc = cleared("e_sc")
        x_wd = load_words("x_wd", x_words)
        offs_t = load_list("offs_t", offs)
        u_t = keep.tile([P, PACK], F32, name="u_t")
        nc.sync.dma_start(u_t[:], unit.rearrange("(p t) o -> p (t o)", t=PACK))
        w1_raw = [load_weight_half("w1a", w1, 0)]
        load_scales(x_sc, x_scales, 0)
        w1_raw.append(load_weight_half("w1b", w1, 1))
        doc_t = load_list("doc_t", doc)
        qa_t = load_list("qa_t", qa)
        load_scales(e_sc, e_scales, E_ROW)
        e_wd = load_words("e_wd", e_words)
        qb_t = load_list("qb_t", qb)
        w2_raw = [load_weight_half("w2a", w2, 0), load_weight_half("w2b", w2, 1)]
        da_t = load_list("da_t", da)
        db_t = load_list("db_t", db)
        w3_raw = keep.tile([P, PACK, 512], F32, name="w3_raw")
        nc.sync.dma_start(w3_raw[:], w3.rearrange("(p j) c -> p j c", j=PACK))

        banks = [psum.tile([P, 512], F32, name="bank%d" % b) for b in range(8)]

        def dealt_out(grouped, m0, m1):
            return grouped[:].rearrange("p (t m j) -> p m j t", t=PACK, j=PACK)[:, m0:m1]

        def dealt_in(raw):
            return raw[:].rearrange("p j (m t) -> p m j t", t=PACK)

        def quantize(name, grouped, width):
            codes = keep.tile([P, width], U32, name=name + "_codes", align_bytes=64)
            scales = keep.tile([P, width], U8, name=name + "_scales", align_bytes=64)
            nc.vector.quantize_mx(out=codes[:].bitcast(FP8X4), scales=scales[:], in_=grouped)
            return codes, scales

        def quantize_weight(name, grouped):
            codes = keep.tile([P, 512], U32, name=name + "_codes", align_bytes=64)
            scales = keep.tile([P, 512], U8, name=name + "_scales", align_bytes=64)
            for t in range(PACK):
                cols = slice(t * P, (t + 1) * P)
                nc.vector.quantize_mx(out=codes[:, cols].bitcast(FP8X4), scales=scales[:, cols], in_=grouped[:, t * 512 : (t + 1) * 512])
            return codes, scales

        def window(name):
            tile = keep.tile([P, S + SPARE], F32, name=name)
            nc.gpsimd.memset(tile[:, S:], 0.0)
            return tile

        def pick(name, table, lst, dtype):
            tile = keep.tile([P, S], dtype, name=name, align_bytes=64)
            nc.vector.tensor_copy(tile[:], table[:].indirect(lst[:]))
            return tile

        def product(dst, w, t, codes, scales):
            nc.tensor.matmul_mx(
                out=dst,
                lhsT=w[0][:, t * P : (t + 1) * P].bitcast(FP8X4),
                lhsT_scale=w[1][:, t * P : (t + 1) * P],
                rhs=codes.bitcast(FP8X4),
                rhs_scale=scales,
                start=True,
                stop=True,
            )

        w1_g = keep.tile([P, PACK * 512], BF16, name="w1_g", align_bytes=64)
        nc.scalar.copy(dealt_out(w1_g, 0, 64), dealt_in(w1_raw[0]))
        xw_pick = pick("xw_pick", x_wd, offs_t, U32)
        xs_pick = pick("xs_pick", x_sc, offs_t, U8)
        nc.vector.tensor_copy(dealt_out(w1_g, 64, 128), dealt_in(w1_raw[1]))
        w1_q = quantize_weight("w1", w1_g)
        y = []
        for t in range(PACK):
            product(banks[t][:], w1_q, t, xw_pick[:], xs_pick[:])
            yt = window("y%d" % t)
            nc.scalar.copy(yt[:, :S], banks[t][:])
            y.append(yt)

        es_pick = pick("es_pick", e_sc, doc_t, U8)
        ew_pick = pick("ew_pick", e_wd, doc_t, U32)
        sign = keep.tile([P, PACK], F32, name="sign")
        half = keep.tile([P, PACK], F32, name="half")
        size = keep.tile([P, PACK], F32, name="size", tag="late")
        nc.gpsimd.tensor_scalar(half[:], u_t[:], 0.0, 0.5, ALU.is_ge, ALU.subtract)
        w2_g = keep.tile([P, PACK * 512], BF16, name="w2_g", align_bytes=64)
        nc.vector.tensor_copy(dealt_out(w2_g, 0, 64), dealt_in(w2_raw[0]))
        nc.gpsimd.tensor_scalar(sign[:], half[:], 2.0, 0.0, ALU.mult, ALU.add)
        nc.vector.tensor_copy(dealt_out(w2_g, 64, 128), dealt_in(w2_raw[1]))
        nc.gpsimd.tensor_tensor(size[:], u_t[:], sign[:], ALU.mult)
        w2_q = quantize_weight("w2", w2_g)
        ye = []
        for t in range(PACK):
            product(banks[PACK + t][:], w2_q, t, ew_pick[:], es_pick[E_ROW:P, :])
            yt = window("ye%d" % t)
            if t == 0:
                nc.vector.tensor_scalar(yt[:, :S], banks[PACK + t][:], size[:, t : t + 1], None, ALU.mult)
            else:
                nc.scalar.activation(yt[:, :S], banks[PACK + t][:], COPY, scale=size[:, t : t + 1])
            ye.append(yt)
        early = EARLY * CHUNKS[0]
        g_early = keep.tile([P, early], F32, name="g_early")
        g_late = keep.tile([P, 2 * PACK * U - early], F32, name="g_late", tag="late")
        w3_g = keep.tile([P, PACK * 512], BF16, name="w3_g", align_bytes=64)

        def round_w3():
            for h in range(2):
                nc.vector.tensor_tensor(
                    dealt_out(w3_g, 64 * h, 64 * h + 64),
                    dealt_in(w3_raw)[:, 64 * h : 64 * h + 64],
                    sign[:].unsqueeze(1).unsqueeze(3).to_broadcast([P, 64, PACK, PACK]),
                    ALU.mult,
                )

        out_scales = keep.tile([P, U], U8, name="out_scales", align_bytes=64)
        out_rows = out_0.rearrange("(p t) r -> p t r", t=PACK)
        out_words = out_1[0].rearrange("p n t -> p (n t)").bitcast(I32)
        starts = [sum(CHUNKS[:c]) for c in range(len(CHUNKS))]

        def woven(tile):
            return tile[:].rearrange("p (c i t) -> p c t i", i=2, t=PACK)

        def planes(tile):
            return tile.rearrange("p t (c i) -> p c t i", i=2)

        def gathered(t, s, r0, n):
            at = (r0 // S) * 2 * PACK * S + (2 * t + s) * S + r0 % S
            return g_early[:, at : at + n] if at < early else g_late[:, at - early : at - early + n]

        def fetch_questions(r0):
            cols = slice(r0 // 16, (r0 + S) // 16)
            for t in range(PACK):
                for s, ql in enumerate((qa_t, qb_t)):
                    nc.scalar.activation(gathered(t, s, r0, S), y[t][:].indirect(ql[:, cols]), COPY)

        def front(c):
            r0, n = starts[c], CHUNKS[c]
            cols = slice(r0 // 16, (r0 + n) // 16)
            prods = keep.tile([P, 2, PACK, n], F32, name="prods%d" % c, tag="hid1" if c == 2 else "prods%d" % c, align_bytes=64)
            if r0 % S == 0:
                fetch_questions(r0)
            if c < len(CHUNKS) - 1:
                for t in range(PACK):
                    for s, dl in enumerate((da_t, db_t)):
                        nc.vector.tensor_tensor(prods[:, s, t, :], ye[t][:].indirect(dl[:, cols]), gathered(t, s, r0, n), ALU.mult)
                    if c == 0 and t == 1:
                        round_w3()
            else:
                docs = keep.tile([P, PACK, 2, n], F32, name="docs")
                for t in range(PACK):
                    for s, dl in enumerate((da_t, db_t)):
                        nc.scalar.activation(docs[:, t, s, :], ye[t][:].indirect(dl[:, cols]), COPY)
                base = (r0 // S) * 2 * PACK * S - early
                qs = g_late[:, base : base + 2 * PACK * S].rearrange("p (t s r) -> p t s r", t=PACK, s=2)[:, :, :, r0 % S : r0 % S + n]
                nc.vector.tensor_tensor(prods[:].rearrange("p s t r -> p t s r"), docs[:], qs, ALU.mult)
            hid = keep.tile([P, PACK * n], BF16, name="hid%d" % c, align_bytes=64)
            nc.vector.tensor_tensor(woven(hid), planes(prods[:, 0]), planes(prods[:, 1]), ALU.max)
            return hid

        def middle(c, hid, w3_q):
            r0, n = starts[c], CHUNKS[c]
            codes, scales = quantize("hid%d" % c, hid[:], n)
            res = keep.tile([P, PACK, n], F32, name="res%d" % c)
            if n == GROUP:
                for t in range(PACK):
                    product(banks[0][:, t * n : (t + 1) * n], w3_q, t, codes[:], scales[:])
                nc.scalar.copy(res[:], banks[0][:].rearrange("p (t r) -> p t r", t=PACK))
            else:
                for t in range(PACK):
                    bank = banks[PACK * c + t]
                    for g0, g1 in ((0, n),) if n == 512 else ((0, 256), (256, n)):
                        product(bank[:, g0:g1], w3_q, t, codes[:, g0:g1], scales[:, g0:g1])
                    nc.scalar.copy(res[:, t, :], bank[:, :n])
                    if c == 1 and t % 2 == 1:
                        nc.sync.dma_start(out_rows[:, t - 1 : t + 1, r0 : r0 + n], res[:, t - 1 : t + 1, :])
            if c != 1:
                nc.sync.dma_start(out_rows[:, :, r0 : r0 + n], res[:])
            return res

        def round_result(c, res):
            n = CHUNKS[c]
            rounded = keep.tile([P, PACK * n], BF16, name="rounded%d" % c, align_bytes=64)
            cut = (n, 256, 0)[c] // 2
            if cut > 0:
                nc.scalar.copy(woven(rounded)[:, :cut], planes(res[:])[:, :cut])
            if cut < n // 2:
                nc.vector.tensor_copy(woven(rounded)[:, cut:], planes(res[:])[:, cut:])
            return rounded

        def back(c, rounded):
            r0, n = starts[c], CHUNKS[c]
            codes = keep.tile([P, n], U32, name="out_codes%d" % c, tag="hid2" if c == 0 else "out_codes%d" % c, align_bytes=64)
            nc.vector.quantize_mx(out=codes[:].bitcast(FP8X4), scales=out_scales[:, r0 : r0 + n], in_=rounded[:])
            nc.sync.dma_start(out_words[:, r0 : r0 + n], codes[:].bitcast(I32))

        hid = front(0)
        w3_q = quantize("w3", w3_g[:], 512)
        res0 = middle(0, hid, w3_q)
        rounded0 = round_result(0, res0)
        res1 = middle(1, front(1), w3_q)
        res2 = middle(2, front(2), w3_q)
        back(0, rounded0)
        back(1, round_result(1, res1))
        back(2, round_result(2, res2))
        for q in range(4):
            eng = nc.sync if q % 2 == 0 else nc.scalar
            eng.dma_start(out_2[0, 4 * q : 4 * q + 4, :].bitcast(I32), out_scales[32 * q : 32 * q + 4, :].bitcast(I32))
